import numpy as np
import ml_dtypes


def mxq(x, axis, fmt="e4m3"):
    dtype, down = {"e4m3": (ml_dtypes.float8_e4m3fn, 7), "e5m2": (ml_dtypes.float8_e5m2, 14)}[fmt]
    v = np.moveaxis(np.asarray(x, np.float32).astype(ml_dtypes.bfloat16).astype(np.float64), axis, -1)
    blocks = v.reshape(v.shape[:-1] + (-1, 32))
    amax = np.abs(blocks).max(-1, keepdims=True)
    byte = np.maximum(np.where(amax > 0, np.frexp(amax)[1] - 1 + 127, 0) - down, 1)
    scale = np.exp2(byte - 127.0)
    codes = (blocks / scale).astype(np.float32).astype(dtype).astype(np.float64)
    return np.moveaxis((codes * scale).reshape(v.shape), -1, axis)


WIDE = False


def mx_kscale(k):
    if not WIDE:
        return np.ones(k)
    levels = np.array([10, -10, 5, -5, 0])
    if k % 512:
        return np.exp2(np.random.permutation(np.resize(levels, k // 32))).repeat(32)
    a = np.empty((k // 512, 16))
    for p in range(k // 512):
        a[p, :8] = np.random.permutation(np.resize(levels, 8))
        for g in range(8):
            far = levels[np.abs(levels - a[p, g]) >= 10]
            a[p, g + 8] = far[np.random.randint(len(far))]
    return np.exp2(a.ravel()).repeat(32)


def f64(x):
    return np.asarray(x).astype(np.float64)


def striped(idx):
    return np.tile(np.asarray(idx).reshape(-1, 16).T, (8, 1)).astype(np.uint16)


def unstriped(offs):
    return offs[:16].T.reshape(-1).astype(np.int64)


E2M1 = np.array([0.0, 0.5, 1.0, 1.5, 2.0, 3.0, 4.0, 6.0, -0.0, -0.5, -1.0, -1.5, -2.0, -3.0, -4.0, -6.0])


def pack_weight(w, fmt):
    k, n = w.shape
    w = f64(np.asarray(w, np.float32).astype(ml_dtypes.bfloat16)).reshape(k // 32, 32, n)
    amax = np.abs(w).max(1)
    if fmt == "e4m3":
        byte = np.frexp(amax)[1] - 1 + 127 - 7
    else:
        mant, ex = np.frexp(amax / 6.0)
        byte = np.where(mant > 0.5, ex, ex - 1) + 127
    byte = np.clip(np.where(amax > 0, byte, 1), 1, 254)
    scaled = (w * np.exp2(127.0 - byte)[:, None, :]).reshape(k, n).astype(np.float32)
    by_word = np.ascontiguousarray(scaled.reshape(k // 512, 128, 4, n).transpose(0, 1, 3, 2))
    if fmt == "e4m3":
        words = by_word.astype(ml_dtypes.float8_e4m3fn).view(np.uint8)
    else:
        c = by_word.astype(ml_dtypes.float4_e2m1fn).view(np.uint8) & 0xF
        words = (c[..., 0::2] | (c[..., 1::2] << 4)).reshape(k // 512, 128, 2 * n)
    return np.ascontiguousarray(words), np.ascontiguousarray(byte.astype(np.uint8).reshape(k // 512, 16, n))


def unpack_weight(words, scales, fmt):
    g, _, n = scales.shape
    words = np.ascontiguousarray(words).reshape(g, 128, n, -1)
    if fmt == "e4m3":
        vals = words.view(ml_dtypes.float8_e4m3fn).astype(np.float64)
    else:
        nib = np.empty((g, 128, n, 4), np.uint8)
        nib[..., 0::2] = words & 0xF
        nib[..., 1::2] = words >> 4
        vals = E2M1[nib]
    vals = vals * np.repeat(np.exp2(scales.astype(np.float64) - 127.0), 8, axis=1)[..., None]
    return vals.transpose(0, 1, 3, 2).reshape(g * 512, n)


D, E, T, I, Q = 512, 512, 2048, 512, 128


def setup_inputs():
    n = np.random.standard_normal
    idx2 = np.random.permutation(I)[:I]
    idx = np.random.permutation(T)[:I]
    fd = mx_kscale(D)
    fe = mx_kscale(E)
    keysp = pack_weight(n((D, T)) / fd[:, None], "e2m1")
    valsp = pack_weight(n((E, T)) / fe[:, None], "e2m1")
    return {
        "query": (n((D, Q)) * 0.8 / np.sqrt(D) * fd[:, None]).astype(np.float32),
        "keys_words": keysp[0],
        "keys_scales": keysp[1],
        "reserve": (np.random.uniform(0.5, 2.0, (Q, 1))).astype(np.float32),
        "gout": (n((E, Q)) * 1 / np.sqrt(E) * fe[:, None]).astype(np.float32),
        "vals_words": valsp[0],
        "vals_scales": valsp[1],
        "base": (0.5 * n((Q, I))).astype(np.float32),
        "offs2": striped(idx2),
        "offs": striped(idx),
    }


def reference(query, keys_words, keys_scales, reserve, gout, vals_words, vals_scales, base, offs2, offs):
    idx2 = unstriped(offs2)
    idx = unstriped(offs)
    keysu = unpack_weight(keys_words, keys_scales, "e2m1")
    valsu = unpack_weight(vals_words, vals_scales, "e2m1")
    queryq = mxq(f64(query), 0, "e4m3")
    keysidxg = keysu[:, idx]
    a = queryq.T @ keysidxg
    p = np.exp(a)
    z = np.sum(p, axis=1, keepdims=True)
    r = p / (p + p[:, idx2] + f64(reserve))
    goutq = mxq(f64(gout), 0, "e4m3")
    valsidxg = valsu[:, idx]
    c0 = goutq.T @ valsidxg
    dr = c0 * p / z
    dz = np.sum(c0 * r * p / np.square(z) * (-1.0), axis=1, keepdims=True)
    e1 = dr * p / np.square(p + p[:, idx2] + f64(reserve)) * (-1.0)
    s1 = np.zeros((Q, I))
    s1[:, idx2] = e1
    dp = c0 * r / z + dr / (p + p[:, idx2] + f64(reserve)) + dz + s1 - dr * p / np.square(p + p[:, idx2] + f64(reserve))
    da = dp * p
    hda = da * 512.0 * 2.0 * 512.0
    hdp = hda * p
    he1 = hdp[:, idx2]
    hdz = np.sum(hdp, axis=1, keepdims=True)
    hdr = hdp / (p + p[:, idx2] + f64(reserve)) + hdp * (-1.0) / np.square(p + p[:, idx2] + f64(reserve)) * p + he1 * (-1.0) / np.square(p + p[:, idx2] + f64(reserve)) * p
    hr = hdp / z * c0 + hdz * (-1.0) / np.square(z) * p * c0
    hz = np.sum(hdp * c0 * r / np.square(z) * (-1.0), axis=1, keepdims=True) + np.sum(hdz * (-1.0) * c0 * r * p / np.square(np.square(z)) * (-1.0), axis=1, keepdims=True) * z * 2.0 + np.sum(hdr * c0 * p / np.square(z) * (-1.0), axis=1, keepdims=True)
    e51 = hdp * dr / np.square(p + p[:, idx2] + f64(reserve)) * (-1.0)
    s51 = np.zeros((Q, I))
    s51[:, idx2] = e51
    e52 = hdp * (-1.0) * dr * p / np.square(np.square(p + p[:, idx2] + f64(reserve))) * (-1.0) * (p + p[:, idx2] + f64(reserve)) * 2.0
    s52 = np.zeros((Q, I))
    s52[:, idx2] = e52
    e53 = he1 * (-1.0) * dr * p / np.square(np.square(p + p[:, idx2] + f64(reserve))) * (-1.0) * (p + p[:, idx2] + f64(reserve)) * 2.0
    s53 = np.zeros((Q, I))
    s53[:, idx2] = e53
    e54 = hr * p / np.square(p + p[:, idx2] + f64(reserve)) * (-1.0)
    s54 = np.zeros((Q, I))
    s54[:, idx2] = e54
    hp = hda * dp + hdp * (-1.0) / np.square(p + p[:, idx2] + f64(reserve)) * dr + hdp * (-1.0) * dr * p / np.square(np.square(p + p[:, idx2] + f64(reserve))) * (-1.0) * (p + p[:, idx2] + f64(reserve)) * 2.0 + he1 * (-1.0) / np.square(p + p[:, idx2] + f64(reserve)) * dr + he1 * (-1.0) * dr * p / np.square(np.square(p + p[:, idx2] + f64(reserve))) * (-1.0) * (p + p[:, idx2] + f64(reserve)) * 2.0 + hdz * (-1.0) / np.square(z) * c0 * r + hdr * c0 / z + hr / (p + p[:, idx2] + f64(reserve)) + hz + s51 + s52 + s53 + s54 - hdp * dr / np.square(p + p[:, idx2] + f64(reserve)) - hr * p / np.square(p + p[:, idx2] + f64(reserve))
    ha = hp * p
    y = ha + f64(base)
    return y

@@ -1,0 +1,161 @@
+from contextlib import ExitStack
+
+import concourse.mybir as mybir
+
+F32 = mybir.dt.float32
+BF16 = mybir.dt.bfloat16
+I32 = mybir.dt.int32
+U32 = mybir.dt.uint32
+U16 = mybir.dt.uint16
+U8 = mybir.dt.uint8
+FP8X4 = mybir.dt.float8_e4m3fn_x4
+FP4X4 = mybir.dt.float4_e2m1fn_x4
+ACT = mybir.ActivationFunctionType
+MULT = mybir.AluOpType.mult
+ADD = mybir.AluOpType.add
+SUB = mybir.AluOpType.subtract
+
+P = 128
+PACK = 4
+POOL = 2048
+SLOTS = 512
+HALF = SLOTS // 2
+PENALTY = 512.0 * 2.0 * 512.0
+FLOPS = 2 * 2 * 512 * 128 * 512
+
+
+def tile_attend_gpneighbourshare_kernel(tc, query, keys_words, keys_scales, reserve, gout, vals_words, vals_scales, base, offs2, offs, out):
+    nc = tc.nc
+    halves = [slice(0, HALF), slice(HALF, SLOTS)]
+    list_halves = [slice(0, HALF // 16), slice(HALF // 16, SLOTS // 16)]
+
+    with ExitStack() as ctx:
+        sb = ctx.enter_context(tc.tile_pool(name="sb", bufs=1))
+        psum = ctx.enter_context(tc.psum_pool(name="psum", bufs=1))
+
+        def row(name):
+            return sb.tile([P, SLOTS], F32, name=name, align_bytes=64)
+
+        def col(name):
+            return sb.tile([P, 1], F32, name=name)
+
+        tokens = sb.tile([P, SLOTS // 16], U16, name="tokens")
+        links = sb.tile([P, SLOTS // 16], U16, name="links")
+        k_words = sb.tile([P, POOL], U16, name="k_words", align_bytes=64)
+        v_words = sb.tile([P, POOL], U16, name="v_words", align_bytes=64)
+        k_bytes = sb.tile([P, POOL], U8, name="k_bytes", align_bytes=64)
+        v_bytes = sb.tile([P, POOL], U8, name="v_bytes", align_bytes=64)
+        q_raw = sb.tile([P, PACK, P], F32, name="q_raw", align_bytes=64)
+        g_raw = sb.tile([P, PACK, P], F32, name="g_raw", align_bytes=64)
+        res = col("res")
+        base_sb = row("base_sb")
+
+        def load_bytes(tile, scales):
+            for quad in range(4):
+                nc.sync.dma_start(tile[32 * quad : 32 * quad + 4, :].bitcast(I32), scales[0, 4 * quad : 4 * quad + 4, :].bitcast(I32))
+
+        nc.vector.memset(k_bytes[:].bitcast(I32), 0)
+        nc.vector.memset(v_bytes[:].bitcast(I32), 0)
+        nc.sync.dma_start(tokens[:], offs)
+        load_bytes(k_bytes, keys_scales)
+        nc.sync.dma_start(k_words[:].bitcast(I32), keys_words[0].bitcast(I32))
+        nc.sync.dma_start(q_raw[:], query.rearrange("(p j) w -> p j w", j=PACK))
+        nc.sync.dma_start(v_words[:].bitcast(I32), vals_words[0].bitcast(I32))
+        load_bytes(v_bytes, vals_scales)
+        nc.sync.dma_start(g_raw[:], gout.rearrange("(p j) w -> p j w", j=PACK))
+        nc.sync.dma_start(links[:], offs2)
+        nc.sync.dma_start(res[:], reserve)
+        nc.sync.dma_start(base_sb[:], base)
+
+        def product(name, raw, words, scale_bytes):
+            grouped = sb.tile([P, P, PACK], BF16, name=name + "_grouped", align_bytes=64)
+            codes = sb.tile([P, P], U32, name=name + "_codes", align_bytes=64)
+            plane = sb.tile([P, P], U8, name=name + "_plane", align_bytes=64)
+            picked_words = sb.tile([P, SLOTS], U16, name=name + "_picked_words", align_bytes=64)
+            picked_bytes = sb.tile([P, SLOTS], U8, name=name + "_picked_bytes", align_bytes=64)
+            acc = psum.tile([P, SLOTS], F32, name=name + "_acc")
+            nc.scalar.activation(grouped[:], raw[:].rearrange("p j w -> p w j"), ACT.Copy)
+            nc.vector.tensor_copy(picked_bytes[:], scale_bytes[:].indirect(tokens[:]))
+            nc.vector.tensor_copy(picked_words[:], words[:].indirect(tokens[:]))
+            nc.vector.quantize_mx(out=codes[:].bitcast(FP8X4), scales=plane[:], in_=grouped[:].rearrange("p w j -> p (w j)"))
+            nc.tensor.matmul_mx(out=acc[:], lhsT=codes[:].bitcast(FP8X4), lhsT_scale=plane[:], rhs=picked_words[:].bitcast(FP4X4), rhs_scale=picked_bytes[:], start=True, stop=True)
+            return acc
+
+        a = product("a", q_raw, k_words, k_bytes)
+        p = row("p")
+        z = col("z")
+        nc.scalar.activation(p[:], a[:], ACT.Exp, accum_out=z[:])
+        c = product("c", g_raw, v_words, v_bytes)
+
+        iz = col("iz")
+        niz = col("niz")
+        nc.vector.reciprocal(iz[:], z[:])
+        nc.vector.tensor_scalar(niz[:], iz[:], -1.0, None, MULT)
+
+        gp, n, s, u, p2 = row("gp"), row("n"), row("s"), row("u"), row("p2")
+        for h, lh in zip(halves, list_halves):
+            nc.vector.tensor_copy(gp[:, h], p[:].indirect(links[:, lh]))
+        for h in halves:
+            nc.vector.scalar_tensor_tensor(n[:, h], gp[:, h], res[:], p[:, h], ADD, ADD)
+        for h in halves:
+            nc.scalar.activation(s[:, h], n[:, h], ACT.Abs_reciprocal_sqrt)
+        for h in halves:
+            nc.scalar.activation(u[:, h], s[:, h], ACT.Square)
+        nc.scalar.activation(p2[:], p[:], ACT.Square)
+
+        r, na, e1, s1 = row("r"), row("na"), row("e1"), row("s1")
+        for h in halves:
+            nc.vector.tensor_tensor(r[:, h], p[:, h], u[:, h], MULT)
+        for h in halves:
+            nc.vector.scalar_tensor_tensor(na[:, h], c[:, h], niz[:], r[:, h], MULT, MULT)
+        for h in halves:
+            nc.vector.tensor_tensor(e1[:, h], na[:, h], r[:, h], MULT)
+        for h, lh in zip(halves, list_halves):
+            nc.scalar.activation(s1[:].indirect(links[:, lh]), e1[:, h], ACT.Copy)
+
+        apn, m, jn, jn2, e2 = row("apn"), row("m"), row("jn"), row("jn2"), row("e2")
+        sn, dz = col("sn"), col("dz")
+        nc.vector.scalar_tensor_tensor(apn[:], na[:], 1.0, p[:], MULT, MULT, accum_out=sn[:])
+        nc.vector.tensor_tensor(jn[:], na[:], e1[:], SUB)
+        nc.vector.scalar_tensor_tensor(m[:], na[:], -2.0, e1[:], MULT, ADD)
+        nc.vector.tensor_scalar(dz[:], sn[:], iz[:], None, MULT)
+        nc.vector.scalar_tensor_tensor(jn2[:], jn[:], 2.0, u[:], MULT, MULT)
+        nc.vector.scalar_tensor_tensor(e2[:], e1[:], 2.0, u[:], MULT, MULT)
+
+        dp, hdp = row("dp"), row("hdp")
+        hsum = [col("hsum0"), col("hsum1")]
+        for h in halves:
+            nc.vector.scalar_tensor_tensor(dp[:, h], s1[:, h], dz[:], m[:, h], ADD, ADD)
+        for h, hs in zip(halves, hsum):
+            nc.vector.scalar_tensor_tensor(hdp[:, h], dp[:, h], PENALTY, p2[:, h], MULT, MULT, accum_out=hs[:])
+
+        he1, y, y2, zz, e5, s5 = row("he1"), row("y"), row("y2"), row("zz"), row("e5"), row("s5")
+        beta, nbeta = col("beta"), col("nbeta")
+        for h, lh in zip(halves, list_halves):
+            nc.scalar.activation(he1[:, h], hdp[:].indirect(links[:, lh]), ACT.Copy)
+        nc.vector.tensor_tensor(y[:, halves[0]], hdp[:, halves[0]], jn2[:, halves[0]], MULT)
+        nc.vector.tensor_scalar(nbeta[:], hsum[0][:], hsum[1][:], niz[:], ADD, MULT)
+        nc.vector.tensor_tensor(y[:, halves[1]], hdp[:, halves[1]], jn2[:, halves[1]], MULT)
+        nc.vector.tensor_scalar(beta[:], hsum[0][:], hsum[1][:], iz[:], ADD, MULT)
+        for h in halves:
+            nc.vector.scalar_tensor_tensor(y2[:, h], e1[:, h], nbeta[:], y[:, h], MULT, ADD)
+            nc.vector.tensor_tensor(zz[:, h], he1[:, h], e2[:, h], MULT)
+        for h in halves:
+            nc.vector.tensor_tensor(e5[:, h], y2[:, h], zz[:, h], SUB)
+        for h, lh in zip(halves, list_halves):
+            nc.scalar.activation(s5[:].indirect(links[:, lh]), e5[:, h], ACT.Copy)
+
+        hh, g1, qe, g3, g4, t, y_out = row("hh"), row("g1"), row("qe"), row("g3"), row("g4"), row("t"), row("y_out")
+        sh, w, hz = col("sh"), col("w"), col("hz")
+        nc.vector.scalar_tensor_tensor(hh[:], hdp[:], 1.0, dp[:], MULT, MULT, accum_out=sh[:])
+        nc.vector.tensor_scalar(w[:], nbeta[:], dz[:], None, MULT)
+        nc.vector.scalar_tensor_tensor(g1[:], apn[:], beta[:], base_sb[:], MULT, ADD)
+        nc.vector.scalar_tensor_tensor(qe[:], gp[:], res[:], e5[:], ADD, MULT)
+        nc.vector.tensor_scalar(hz[:], sh[:], niz[:], w[:], MULT, ADD)
+        nc.vector.tensor_tensor(g3[:], g1[:], hh[:], ADD)
+        nc.vector.tensor_tensor(g4[:], g3[:], qe[:], SUB)
+        for h in halves:
+            nc.vector.scalar_tensor_tensor(t[:, h], s5[:, h], hz[:], p[:, h], ADD, MULT)
+        for h in halves:
+            nc.vector.tensor_tensor(y_out[:, h], t[:, h], g4[:, h], ADD)
+            nc.sync.dma_start(out[:, h], y_out[:, h])

@@ -42,118 +42,132 @@ def tile_attend_gpneighbourshare_kernel(tc, query, keys_words, keys_scales, rese
         tokens = sb.tile([P, SLOTS // 16], U16, name="tokens")
         links = sb.tile([P, SLOTS // 16], U16, name="links")
         k_words = sb.tile([P, POOL], U16, name="k_words", align_bytes=64)
-        v_words = sb.tile([P, POOL], U16, name="v_words", align_bytes=64)
-        k_bytes = sb.tile([P, POOL], U8, name="k_bytes", align_bytes=64)
+        k_bytes = sb.tile([P, POOL], U8, name="k_bytes", tag="second", align_bytes=64)
         v_bytes = sb.tile([P, POOL], U8, name="v_bytes", align_bytes=64)
-        q_raw = sb.tile([P, PACK, P], F32, name="q_raw", align_bytes=64)
+        q_raw = sb.tile([P, PACK, P], F32, name="q_raw", tag="first", align_bytes=64)
         g_raw = sb.tile([P, PACK, P], F32, name="g_raw", align_bytes=64)
         res = col("res")
-        base_sb = row("base_sb")
 
         def load_bytes(tile, scales):
             for quad in range(4):
                 nc.sync.dma_start(tile[32 * quad : 32 * quad + 4, :].bitcast(I32), scales[0, 4 * quad : 4 * quad + 4, :].bitcast(I32))
 
-        nc.vector.memset(k_bytes[:].bitcast(I32), 0)
+        nc.gpsimd.memset(k_bytes[:].bitcast(I32), 0)
         nc.vector.memset(v_bytes[:].bitcast(I32), 0)
+        nc.scalar.dma_start(q_raw[:], query.rearrange("(p j) w -> p j w", j=PACK))
+        nc.gpsimd.dma_start(g_raw[:], gout.rearrange("(p j) w -> p j w", j=PACK))
+        nc.gpsimd.dma_start(res[:], reserve)
         nc.sync.dma_start(tokens[:], offs)
-        load_bytes(k_bytes, keys_scales)
         nc.sync.dma_start(k_words[:].bitcast(I32), keys_words[0].bitcast(I32))
-        nc.sync.dma_start(q_raw[:], query.rearrange("(p j) w -> p j w", j=PACK))
-        nc.sync.dma_start(v_words[:].bitcast(I32), vals_words[0].bitcast(I32))
-        load_bytes(v_bytes, vals_scales)
-        nc.sync.dma_start(g_raw[:], gout.rearrange("(p j) w -> p j w", j=PACK))
+        load_bytes(k_bytes, keys_scales)
         nc.sync.dma_start(links[:], offs2)
-        nc.sync.dma_start(res[:], reserve)
-        nc.sync.dma_start(base_sb[:], base)
+        load_bytes(v_bytes, vals_scales)
 
-        def product(name, raw, words, scale_bytes):
+        def quantise(name, raw):
             grouped = sb.tile([P, P, PACK], BF16, name=name + "_grouped", align_bytes=64)
             codes = sb.tile([P, P], U32, name=name + "_codes", align_bytes=64)
             plane = sb.tile([P, P], U8, name=name + "_plane", align_bytes=64)
-            picked_words = sb.tile([P, SLOTS], U16, name=name + "_picked_words", align_bytes=64)
-            picked_bytes = sb.tile([P, SLOTS], U8, name=name + "_picked_bytes", align_bytes=64)
-            acc = psum.tile([P, SLOTS], F32, name=name + "_acc")
             nc.scalar.activation(grouped[:], raw[:].rearrange("p j w -> p w j"), ACT.Copy)
-            nc.vector.tensor_copy(picked_bytes[:], scale_bytes[:].indirect(tokens[:]))
-            nc.vector.tensor_copy(picked_words[:], words[:].indirect(tokens[:]))
             nc.vector.quantize_mx(out=codes[:].bitcast(FP8X4), scales=plane[:], in_=grouped[:].rearrange("p w j -> p (w j)"))
-            nc.tensor.matmul_mx(out=acc[:], lhsT=codes[:].bitcast(FP8X4), lhsT_scale=plane[:], rhs=picked_words[:].bitcast(FP4X4), rhs_scale=picked_bytes[:], start=True, stop=True)
+            return codes, plane
+
+        def pick(name, window, dtype, tag):
+            picked = sb.tile([P, SLOTS], dtype, name=name, tag=tag, align_bytes=64)
+            nc.vector.tensor_copy(picked[:], window[:].indirect(tokens[:]))
+            return picked
+
+        def product(name, codes, plane, words, scale_bytes):
+            acc = psum.tile([P, SLOTS], F32, name=name)
+            nc.tensor.matmul_mx(out=acc[:], lhsT=codes[:].bitcast(FP8X4), lhsT_scale=plane[:], rhs=words[:].bitcast(FP4X4), rhs_scale=scale_bytes[:], start=True, stop=True)
             return acc
 
-        a = product("a", q_raw, k_words, k_bytes)
-        p = row("p")
-        z = col("z")
+        lo, hi = halves
+        list_lo, list_hi = list_halves
+        kw = pick("kw", k_words, U16, "kw")
+        q_codes, q_plane = quantise("q", q_raw)
+        v_words = sb.tile([P, POOL], U16, name="v_words", tag="first", align_bytes=64)
+        nc.sync.dma_start(v_words[:].bitcast(I32), vals_words[0].bitcast(I32))
+        kb = pick("kb", k_bytes, U8, "kb")
+        base_sb = sb.tile([P, SLOTS], F32, name="base_sb", tag="second", align_bytes=64)
+        nc.sync.dma_start(base_sb[:], base)
+        a = product("a", q_codes, q_plane, kw, kb)
+        g_codes, g_plane = quantise("g", g_raw)
+        p, p_twin = row("p"), row("p_twin")
+        z, iz, niz2 = col("z"), col("iz"), col("niz2")
+        r = row("r")
+        niz = [r[:, HALF : HALF + 1], col("niz")[:]]
         nc.scalar.activation(p[:], a[:], ACT.Exp, accum_out=z[:])
-        c = product("c", g_raw, v_words, v_bytes)
+        nc.scalar.activation(p_twin[:], a[:], ACT.Exp)
+        sz, hiz = col("sz"), col("hiz")
+        nc.scalar.activation(sz[:], z[:], ACT.Abs_reciprocal_sqrt)
+        for scaled, factor in ((niz[0], -1.0), (niz[1], -1.0), (iz[:], 1.0), (hiz[:], 0.5), (niz2[:], -2.0)):
+            nc.gpsimd.tensor_scalar(scaled, sz[:], sz[:], factor, MULT, MULT)
+        vb = pick("vb", v_bytes, U8, "k_words")
+        vw = pick("vw", v_words, U16, "vw")
+        c = product("c", g_codes, g_plane, vw, vb)
 
-        iz = col("iz")
-        niz = col("niz")
-        nc.vector.reciprocal(iz[:], z[:])
-        nc.vector.tensor_scalar(niz[:], iz[:], -1.0, None, MULT)
-
-        gp, n, s, u, p2 = row("gp"), row("n"), row("s"), row("u"), row("p2")
+        n = sb.tile([P, SLOTS], F32, name="n", tag="first", align_bytes=64)
+        u = row("u")
+        s = sb.tile([P, HALF], F32, name="s")
         for h, lh in zip(halves, list_halves):
-            nc.vector.tensor_copy(gp[:, h], p[:].indirect(links[:, lh]))
+            nc.vector.tensor_tensor(n[:, h], p[:].indirect(links[:, lh]), p_twin[:, h], ADD)
         for h in halves:
-            nc.vector.scalar_tensor_tensor(n[:, h], gp[:, h], res[:], p[:, h], ADD, ADD)
-        for h in halves:
-            nc.scalar.activation(s[:, h], n[:, h], ACT.Abs_reciprocal_sqrt)
-        for h in halves:
-            nc.scalar.activation(u[:, h], s[:, h], ACT.Square)
-        nc.scalar.activation(p2[:], p[:], ACT.Square)
+            nc.scalar.activation(s[:], n[:, h], ACT.Abs_reciprocal_sqrt, bias=res[:])
+            nc.scalar.activation(u[:, h], s[:], ACT.Square)
 
-        r, na, e1, s1 = row("r"), row("na"), row("e1"), row("s1")
-        for h in halves:
-            nc.vector.tensor_tensor(r[:, h], p[:, h], u[:, h], MULT)
-        for h in halves:
-            nc.vector.scalar_tensor_tensor(na[:, h], c[:, h], niz[:], r[:, h], MULT, MULT)
-        for h in halves:
-            nc.vector.tensor_tensor(e1[:, h], na[:, h], r[:, h], MULT)
-        for h, lh in zip(halves, list_halves):
-            nc.scalar.activation(s1[:].indirect(links[:, lh]), e1[:, h], ACT.Copy)
-
-        apn, m, jn, jn2, e2 = row("apn"), row("m"), row("jn"), row("jn2"), row("e2")
+        apn, na, e1, s1 = row("apn"), row("na"), row("e1"), row("s1")
+        m, jn = row("m"), row("jn")
         sn, dz = col("sn"), col("dz")
+        for h, lh, minus_iz in zip(halves, list_halves, niz):
+            nc.vector.tensor_tensor(r[:, h], p[:, h], u[:, h], MULT)
+            nc.vector.scalar_tensor_tensor(na[:, h], c[:, h], minus_iz, r[:, h], MULT, MULT)
+            nc.vector.tensor_tensor(e1[:, h], na[:, h], r[:, h], MULT)
+            nc.scalar.activation(s1[:].indirect(links[:, lh]), e1[:, h], ACT.Copy)
         nc.vector.scalar_tensor_tensor(apn[:], na[:], 1.0, p[:], MULT, MULT, accum_out=sn[:])
-        nc.vector.tensor_tensor(jn[:], na[:], e1[:], SUB)
+        nc.gpsimd.tensor_scalar(dz[:], sn[:], iz[:], 0.0, MULT, ADD)
         nc.vector.scalar_tensor_tensor(m[:], na[:], -2.0, e1[:], MULT, ADD)
-        nc.vector.tensor_scalar(dz[:], sn[:], iz[:], None, MULT)
-        nc.vector.scalar_tensor_tensor(jn2[:], jn[:], 2.0, u[:], MULT, MULT)
-        nc.vector.scalar_tensor_tensor(e2[:], e1[:], 2.0, u[:], MULT, MULT)
+        nc.vector.tensor_tensor(jn[:], na[:], e1[:], SUB)
 
-        dp, hdp = row("dp"), row("hdp")
+        dp = na
+        da, hdp, hh = row("da"), row("hdp"), row("hh")
         hsum = [col("hsum0"), col("hsum1")]
+        sh = col("sh")
         for h in halves:
             nc.vector.scalar_tensor_tensor(dp[:, h], s1[:, h], dz[:], m[:, h], ADD, ADD)
-        for h, hs in zip(halves, hsum):
-            nc.vector.scalar_tensor_tensor(hdp[:, h], dp[:, h], PENALTY, p2[:, h], MULT, MULT, accum_out=hs[:])
+        for h in halves:
+            nc.vector.tensor_tensor(da[:, h], dp[:, h], p[:, h], MULT)
+        for h, acc in zip(halves, hsum):
+            nc.vector.scalar_tensor_tensor(hdp[:, h], da[:, h], PENALTY, p[:, h], MULT, MULT, accum_out=acc[:])
+        nc.scalar.activation(hh[:], da[:], ACT.Square, scale=512.0, accum_out=sh[:])
 
-        he1, y, y2, zz, e5, s5 = row("he1"), row("y"), row("y2"), row("zz"), row("e5"), row("s5")
-        beta, nbeta = col("beta"), col("nbeta")
+        he1, y, y2, zz, fn, e5, s5 = row("he1"), row("y"), row("y2"), row("zz"), row("fn"), row("e5"), row("s5")
+        hbeta, beta = col("hbeta"), col("beta")
         for h, lh in zip(halves, list_halves):
             nc.scalar.activation(he1[:, h], hdp[:].indirect(links[:, lh]), ACT.Copy)
-        nc.vector.tensor_tensor(y[:, halves[0]], hdp[:, halves[0]], jn2[:, halves[0]], MULT)
-        nc.vector.tensor_scalar(nbeta[:], hsum[0][:], hsum[1][:], niz[:], ADD, MULT)
-        nc.vector.tensor_tensor(y[:, halves[1]], hdp[:, halves[1]], jn2[:, halves[1]], MULT)
-        nc.vector.tensor_scalar(beta[:], hsum[0][:], hsum[1][:], iz[:], ADD, MULT)
-        for h in halves:
-            nc.vector.scalar_tensor_tensor(y2[:, h], e1[:, h], nbeta[:], y[:, h], MULT, ADD)
-            nc.vector.tensor_tensor(zz[:, h], he1[:, h], e2[:, h], MULT)
-        for h in halves:
-            nc.vector.tensor_tensor(e5[:, h], y2[:, h], zz[:, h], SUB)
-        for h, lh in zip(halves, list_halves):
-            nc.scalar.activation(s5[:].indirect(links[:, lh]), e5[:, h], ACT.Copy)
-
-        hh, g1, qe, g3, g4, t, y_out = row("hh"), row("g1"), row("qe"), row("g3"), row("g4"), row("t"), row("y_out")
-        sh, w, hz = col("sh"), col("w"), col("hz")
-        nc.vector.scalar_tensor_tensor(hh[:], hdp[:], 1.0, dp[:], MULT, MULT, accum_out=sh[:])
-        nc.vector.tensor_scalar(w[:], nbeta[:], dz[:], None, MULT)
-        nc.vector.scalar_tensor_tensor(g1[:], apn[:], beta[:], base_sb[:], MULT, ADD)
-        nc.vector.scalar_tensor_tensor(qe[:], gp[:], res[:], e5[:], ADD, MULT)
-        nc.vector.tensor_scalar(hz[:], sh[:], niz[:], w[:], MULT, ADD)
-        nc.vector.tensor_tensor(g3[:], g1[:], hh[:], ADD)
-        nc.vector.tensor_tensor(g4[:], g3[:], qe[:], SUB)
+        nc.vector.tensor_tensor(y[:, lo], hdp[:, lo], jn[:, lo], MULT)
+        nc.vector.tensor_scalar(hbeta[:], hsum[0][:], hsum[1][:], hiz[:], ADD, MULT)
+        nc.gpsimd.tensor_scalar(beta[:], hsum[0][:], hsum[1][:], iz[:], ADD, MULT)
+        nc.vector.tensor_tensor(y[:, hi], hdp[:, hi], jn[:, hi], MULT)
+        nc.vector.scalar_tensor_tensor(y2[:, lo], apn[:, lo], hbeta[:], y[:, lo], MULT, SUB)
+        nc.vector.tensor_tensor(zz[:, lo], he1[:, lo], e1[:, lo], MULT)
+        nc.vector.scalar_tensor_tensor(y2[:, hi], apn[:, hi], hbeta[:], y[:, hi], MULT, SUB)
+        nc.vector.tensor_tensor(fn[:, lo], zz[:, lo], y2[:, lo], ADD)
+        nc.vector.tensor_tensor(zz[:, hi], he1[:, hi], e1[:, hi], MULT)
+        nc.vector.scalar_tensor_tensor(e5[:, lo], fn[:, lo], -2.0, u[:, lo], MULT, MULT)
+        nc.scalar.activation(s5[:].indirect(links[:, list_lo]), e5[:, lo], ACT.Copy)
+        nc.vector.tensor_tensor(fn[:, hi], zz[:, hi], y2[:, hi], ADD)
+        g1, g2, g3, g4, y_out = row("g1"), row("g2"), row("g3"), row("g4"), row("y_out")
+        w, hz = col("w"), col("hz")
+        nc.vector.scalar_tensor_tensor(g1[:, lo], apn[:, lo], beta[:], base_sb[:, lo], MULT, ADD)
+        nc.vector.scalar_tensor_tensor(e5[:, hi], fn[:, hi], -2.0, u[:, hi], MULT, MULT)
+        nc.scalar.activation(s5[:].indirect(links[:, list_hi]), e5[:, hi], ACT.Copy)
+        nc.vector.scalar_tensor_tensor(g1[:, hi], apn[:, hi], beta[:], base_sb[:, hi], MULT, ADD)
+        nc.gpsimd.tensor_scalar(w[:], beta[:], dz[:], 0.0, MULT, ADD)
+        nc.gpsimd.tensor_scalar(hz[:], sh[:], niz2[:], w[:], MULT, SUB)
+        nc.vector.scalar_tensor_tensor(g2[:], r[:], 1.0, fn[:], SUB, MULT)
+        nc.vector.scalar_tensor_tensor(g3[:], hh[:], 2.0, g1[:], MULT, ADD)
+        nc.vector.scalar_tensor_tensor(g4[:], g2[:], -2.0, g3[:], MULT, ADD)
+        t = g2
         for h in halves:
             nc.vector.scalar_tensor_tensor(t[:, h], s5[:, h], hz[:], p[:, h], ADD, MULT)
         for h in halves:

@@ -45,17 +45,15 @@ def tile_attend_gpneighbourshare_kernel(tc, query, keys_words, keys_scales, rese
         k_bytes = sb.tile([P, POOL], U8, name="k_bytes", tag="second", align_bytes=64)
         v_bytes = sb.tile([P, POOL], U8, name="v_bytes", align_bytes=64)
         q_raw = sb.tile([P, PACK, P], F32, name="q_raw", tag="first", align_bytes=64)
-        g_raw = sb.tile([P, PACK, P], F32, name="g_raw", align_bytes=64)
         res = col("res")
 
         def load_bytes(tile, scales):
             for quad in range(4):
                 nc.sync.dma_start(tile[32 * quad : 32 * quad + 4, :].bitcast(I32), scales[0, 4 * quad : 4 * quad + 4, :].bitcast(I32))
 
-        nc.gpsimd.memset(k_bytes[:].bitcast(I32), 0)
-        nc.vector.memset(v_bytes[:].bitcast(I32), 0)
+        nc.vector.memset(k_bytes[:].bitcast(I32), 0)
+        nc.gpsimd.memset(v_bytes[:].bitcast(I32), 0)
         nc.scalar.dma_start(q_raw[:], query.rearrange("(p j) w -> p j w", j=PACK))
-        nc.gpsimd.dma_start(g_raw[:], gout.rearrange("(p j) w -> p j w", j=PACK))
         nc.gpsimd.dma_start(res[:], reserve)
         nc.sync.dma_start(tokens[:], offs)
         nc.sync.dma_start(k_words[:].bitcast(I32), keys_words[0].bitcast(I32))
@@ -63,11 +61,11 @@ def tile_attend_gpneighbourshare_kernel(tc, query, keys_words, keys_scales, rese
         nc.sync.dma_start(links[:], offs2)
         load_bytes(v_bytes, vals_scales)
 
-        def quantise(name, raw):
+        def quantise(name, raw, cast):
             grouped = sb.tile([P, P, PACK], BF16, name=name + "_grouped", align_bytes=64)
             codes = sb.tile([P, P], U32, name=name + "_codes", align_bytes=64)
             plane = sb.tile([P, P], U8, name=name + "_plane", align_bytes=64)
-            nc.scalar.activation(grouped[:], raw[:].rearrange("p j w -> p w j"), ACT.Copy)
+            cast(grouped[:], raw[:].rearrange("p j w -> p w j"))
             nc.vector.quantize_mx(out=codes[:].bitcast(FP8X4), scales=plane[:], in_=grouped[:].rearrange("p w j -> p (w j)"))
             return codes, plane
 
@@ -83,90 +81,93 @@ def tile_attend_gpneighbourshare_kernel(tc, query, keys_words, keys_scales, rese
 
         lo, hi = halves
         list_lo, list_hi = list_halves
-        kw = pick("kw", k_words, U16, "kw")
-        q_codes, q_plane = quantise("q", q_raw)
+        kb = pick("kb", k_bytes, U8, "kb")
+        g_raw = sb.tile([P, PACK, P], F32, name="g_raw", tag="second", align_bytes=64)
+        q_codes, q_plane = quantise("q", q_raw, nc.scalar.copy)
         v_words = sb.tile([P, POOL], U16, name="v_words", tag="first", align_bytes=64)
         nc.sync.dma_start(v_words[:].bitcast(I32), vals_words[0].bitcast(I32))
-        kb = pick("kb", k_bytes, U8, "kb")
-        base_sb = sb.tile([P, SLOTS], F32, name="base_sb", tag="second", align_bytes=64)
-        nc.sync.dma_start(base_sb[:], base)
+        nc.sync.dma_start(g_raw[:], gout.rearrange("(p j) w -> p j w", j=PACK))
+        kw = pick("kw", k_words, U16, "kw")
         a = product("a", q_codes, q_plane, kw, kb)
-        g_codes, g_plane = quantise("g", g_raw)
         p, p_twin = row("p"), row("p_twin")
-        z, iz, niz2 = col("z"), col("iz"), col("niz2")
-        r = row("r")
-        niz = [r[:, HALF : HALF + 1], col("niz")[:]]
+        z, sz = col("z"), col("sz")
         nc.scalar.activation(p[:], a[:], ACT.Exp, accum_out=z[:])
         nc.scalar.activation(p_twin[:], a[:], ACT.Exp)
-        sz, hiz = col("sz"), col("hiz")
         nc.scalar.activation(sz[:], z[:], ACT.Abs_reciprocal_sqrt)
-        for scaled, factor in ((niz[0], -1.0), (niz[1], -1.0), (iz[:], 1.0), (hiz[:], 0.5), (niz2[:], -2.0)):
-            nc.gpsimd.tensor_scalar(scaled, sz[:], sz[:], factor, MULT, MULT)
-        vb = pick("vb", v_bytes, U8, "k_words")
+        vb = pick("vb", v_bytes, U8, "vb")
         vw = pick("vw", v_words, U16, "vw")
+        g_codes, g_plane = quantise("g", g_raw, nc.vector.tensor_copy)
         c = product("c", g_codes, g_plane, vw, vb)
+        base_sb = sb.tile([P, SLOTS], F32, name="base_sb", tag="second", align_bytes=64)
+        nc.sync.dma_start(base_sb[:], base)
 
         n = sb.tile([P, SLOTS], F32, name="n", tag="first", align_bytes=64)
         u = row("u")
-        s = sb.tile([P, HALF], F32, name="s")
+        s = sb.tile([P, HALF], F32, name="s", align_bytes=64)
         for h, lh in zip(halves, list_halves):
             nc.vector.tensor_tensor(n[:, h], p[:].indirect(links[:, lh]), p_twin[:, h], ADD)
+        niz = sb.tile([P, 1], F32, name="niz", tag="p_twin", align_bytes=64)
+        nc.vector.tensor_scalar(niz[:], sz[:], sz[:], -1.0, MULT, MULT)
         for h in halves:
             nc.scalar.activation(s[:], n[:, h], ACT.Abs_reciprocal_sqrt, bias=res[:])
             nc.scalar.activation(u[:, h], s[:], ACT.Square)
+        p2 = sb.tile([P, SLOTS], F32, name="p2", tag="s", align_bytes=64)
+        nc.scalar.activation(p2[:], p[:], ACT.Square)
 
-        apn, na, e1, s1 = row("apn"), row("na"), row("e1"), row("s1")
+        r, apn, na, e1, s1 = row("r"), row("apn"), row("na"), row("e1"), row("s1")
         m, jn = row("m"), row("jn")
-        sn, dz = col("sn"), col("dz")
-        for h, lh, minus_iz in zip(halves, list_halves, niz):
-            nc.vector.tensor_tensor(r[:, h], p[:, h], u[:, h], MULT)
-            nc.vector.scalar_tensor_tensor(na[:, h], c[:, h], minus_iz, r[:, h], MULT, MULT)
-            nc.vector.tensor_tensor(e1[:, h], na[:, h], r[:, h], MULT)
-            nc.scalar.activation(s1[:].indirect(links[:, lh]), e1[:, h], ACT.Copy)
-        nc.vector.scalar_tensor_tensor(apn[:], na[:], 1.0, p[:], MULT, MULT, accum_out=sn[:])
-        nc.gpsimd.tensor_scalar(dz[:], sn[:], iz[:], 0.0, MULT, ADD)
-        nc.vector.scalar_tensor_tensor(m[:], na[:], -2.0, e1[:], MULT, ADD)
+        sn = [col("sn0"), col("sn1")]
+        ndz = col("ndz")
+        nc.vector.tensor_tensor(r[:, lo], p[:, lo], u[:, lo], MULT)
+        nc.vector.scalar_tensor_tensor(na[:, lo], c[:, lo], niz[:], r[:, lo], MULT, MULT)
+        nc.vector.tensor_tensor(e1[:, lo], na[:, lo], r[:, lo], MULT)
+        nc.scalar.activation(s1[:].indirect(links[:, list_lo]), e1[:, lo], ACT.Copy)
+        nc.vector.tensor_tensor(r[:, hi], p[:, hi], u[:, hi], MULT)
+        nc.vector.scalar_tensor_tensor(apn[:, lo], na[:, lo], 1.0, p[:, lo], MULT, MULT, accum_out=sn[0][:])
+        nc.vector.scalar_tensor_tensor(na[:, hi], c[:, hi], niz[:], r[:, hi], MULT, MULT)
+        nc.vector.scalar_tensor_tensor(m[:, lo], na[:, lo], -2.0, e1[:, lo], MULT, ADD)
+        nc.vector.tensor_tensor(e1[:, hi], na[:, hi], r[:, hi], MULT)
+        nc.scalar.activation(s1[:].indirect(links[:, list_hi]), e1[:, hi], ACT.Copy)
+        nc.vector.scalar_tensor_tensor(apn[:, hi], na[:, hi], 1.0, p[:, hi], MULT, MULT, accum_out=sn[1][:])
+        nc.vector.scalar_tensor_tensor(m[:, hi], na[:, hi], -2.0, e1[:, hi], MULT, ADD)
+        nc.vector.tensor_scalar(ndz[:], sn[0][:], sn[1][:], niz[:], ADD, MULT)
         nc.vector.tensor_tensor(jn[:], na[:], e1[:], SUB)
 
         dp = na
-        da, hdp, hh = row("da"), row("hdp"), row("hh")
+        hdp, hh = row("hdp"), row("hh")
         hsum = [col("hsum0"), col("hsum1")]
-        sh = col("sh")
         for h in halves:
-            nc.vector.scalar_tensor_tensor(dp[:, h], s1[:, h], dz[:], m[:, h], ADD, ADD)
-        for h in halves:
-            nc.vector.tensor_tensor(da[:, h], dp[:, h], p[:, h], MULT)
+            nc.vector.scalar_tensor_tensor(dp[:, h], s1[:, h], ndz[:], m[:, h], SUB, ADD)
         for h, acc in zip(halves, hsum):
-            nc.vector.scalar_tensor_tensor(hdp[:, h], da[:, h], PENALTY, p[:, h], MULT, MULT, accum_out=acc[:])
-        nc.scalar.activation(hh[:], da[:], ACT.Square, scale=512.0, accum_out=sh[:])
+            nc.vector.scalar_tensor_tensor(hdp[:, h], dp[:, h], PENALTY, p2[:, h], MULT, MULT, accum_out=acc[:])
 
-        he1, y, y2, zz, fn, e5, s5 = row("he1"), row("y"), row("y2"), row("zz"), row("fn"), row("e5"), row("s5")
-        hbeta, beta = col("hbeta"), col("beta")
+        he1, y, y2, zz, f, e5, s5 = row("he1"), row("y"), row("y2"), row("zz"), row("f"), row("e5"), row("s5")
+        g1, g2, g3, g4, y_out = row("g1"), row("g2"), row("g3"), row("g4"), row("y_out")
+        nbeta, sh, w, hz = col("nbeta"), col("sh"), col("w"), col("hz")
         for h, lh in zip(halves, list_halves):
             nc.scalar.activation(he1[:, h], hdp[:].indirect(links[:, lh]), ACT.Copy)
-        nc.vector.tensor_tensor(y[:, lo], hdp[:, lo], jn[:, lo], MULT)
-        nc.vector.tensor_scalar(hbeta[:], hsum[0][:], hsum[1][:], hiz[:], ADD, MULT)
-        nc.gpsimd.tensor_scalar(beta[:], hsum[0][:], hsum[1][:], iz[:], ADD, MULT)
-        nc.vector.tensor_tensor(y[:, hi], hdp[:, hi], jn[:, hi], MULT)
-        nc.vector.scalar_tensor_tensor(y2[:, lo], apn[:, lo], hbeta[:], y[:, lo], MULT, SUB)
-        nc.vector.tensor_tensor(zz[:, lo], he1[:, lo], e1[:, lo], MULT)
-        nc.vector.scalar_tensor_tensor(y2[:, hi], apn[:, hi], hbeta[:], y[:, hi], MULT, SUB)
-        nc.vector.tensor_tensor(fn[:, lo], zz[:, lo], y2[:, lo], ADD)
-        nc.vector.tensor_tensor(zz[:, hi], he1[:, hi], e1[:, hi], MULT)
-        nc.vector.scalar_tensor_tensor(e5[:, lo], fn[:, lo], -2.0, u[:, lo], MULT, MULT)
+        nc.vector.scalar_tensor_tensor(y[:, lo], hdp[:, lo], 2.0, jn[:, lo], MULT, MULT)
+        nc.vector.tensor_scalar(nbeta[:], hsum[0][:], hsum[1][:], niz[:], ADD, MULT)
+        nc.vector.scalar_tensor_tensor(y[:, hi], hdp[:, hi], 2.0, jn[:, hi], MULT, MULT)
+        nc.vector.scalar_tensor_tensor(y2[:, lo], apn[:, lo], nbeta[:], y[:, lo], MULT, ADD)
+        nc.vector.scalar_tensor_tensor(zz[:, lo], he1[:, lo], 2.0, e1[:, lo], MULT, MULT)
+        nc.vector.scalar_tensor_tensor(y2[:, hi], apn[:, hi], nbeta[:], y[:, hi], MULT, ADD)
+        nc.vector.tensor_tensor(f[:, lo], y2[:, lo], zz[:, lo], SUB)
+        nc.vector.scalar_tensor_tensor(zz[:, hi], he1[:, hi], 2.0, e1[:, hi], MULT, MULT)
+        nc.vector.tensor_tensor(e5[:, lo], f[:, lo], u[:, lo], MULT)
         nc.scalar.activation(s5[:].indirect(links[:, list_lo]), e5[:, lo], ACT.Copy)
-        nc.vector.tensor_tensor(fn[:, hi], zz[:, hi], y2[:, hi], ADD)
-        g1, g2, g3, g4, y_out = row("g1"), row("g2"), row("g3"), row("g4"), row("y_out")
-        w, hz = col("w"), col("hz")
-        nc.vector.scalar_tensor_tensor(g1[:, lo], apn[:, lo], beta[:], base_sb[:, lo], MULT, ADD)
-        nc.vector.scalar_tensor_tensor(e5[:, hi], fn[:, hi], -2.0, u[:, hi], MULT, MULT)
+        nc.vector.tensor_tensor(f[:, hi], y2[:, hi], zz[:, hi], SUB)
+        nc.vector.scalar_tensor_tensor(g1[:, lo], apn[:, lo], nbeta[:], base_sb[:, lo], MULT, SUB)
+        nc.vector.tensor_tensor(e5[:, hi], f[:, hi], u[:, hi], MULT)
         nc.scalar.activation(s5[:].indirect(links[:, list_hi]), e5[:, hi], ACT.Copy)
-        nc.vector.scalar_tensor_tensor(g1[:, hi], apn[:, hi], beta[:], base_sb[:, hi], MULT, ADD)
-        nc.gpsimd.tensor_scalar(w[:], beta[:], dz[:], 0.0, MULT, ADD)
-        nc.gpsimd.tensor_scalar(hz[:], sh[:], niz2[:], w[:], MULT, SUB)
-        nc.vector.scalar_tensor_tensor(g2[:], r[:], 1.0, fn[:], SUB, MULT)
-        nc.vector.scalar_tensor_tensor(g3[:], hh[:], 2.0, g1[:], MULT, ADD)
-        nc.vector.scalar_tensor_tensor(g4[:], g2[:], -2.0, g3[:], MULT, ADD)
+        nc.vector.scalar_tensor_tensor(hh[:], hdp[:], 1.0, dp[:], MULT, MULT, accum_out=sh[:])
+        nc.vector.scalar_tensor_tensor(g1[:, hi], apn[:, hi], nbeta[:], base_sb[:, hi], MULT, SUB)
+        nc.vector.tensor_scalar(w[:], nbeta[:], ndz[:], None, MULT)
+        nc.vector.scalar_tensor_tensor(g2[:], r[:], 1.0, f[:], SUB, MULT)
+        nc.vector.tensor_tensor(g3[:], g1[:], hh[:], SUB)
+        nc.vector.tensor_scalar(hz[:], sh[:], niz[:], w[:], MULT, SUB)
+        for h in halves:
+            nc.vector.tensor_tensor(g4[:, h], g2[:, h], g3[:, h], SUB)
         t = g2
         for h in halves:
             nc.vector.scalar_tensor_tensor(t[:, h], s5[:, h], hz[:], p[:, h], ADD, MULT)

from contextlib import ExitStack

import concourse.mybir as mybir

F32 = mybir.dt.float32
BF16 = mybir.dt.bfloat16
I32 = mybir.dt.int32
U32 = mybir.dt.uint32
U16 = mybir.dt.uint16
U8 = mybir.dt.uint8
FP8X4 = mybir.dt.float8_e4m3fn_x4
FP4X4 = mybir.dt.float4_e2m1fn_x4
ACT = mybir.ActivationFunctionType
MULT = mybir.AluOpType.mult
ADD = mybir.AluOpType.add
SUB = mybir.AluOpType.subtract

P = 128
PACK = 4
POOL = 2048
SLOTS = 512
HALF = SLOTS // 2
PENALTY = 512.0 * 2.0 * 512.0
FLOPS = 2 * 2 * 512 * 128 * 512


def tile_attend_gpneighbourshare_kernel(tc, query, keys_words, keys_scales, reserve, gout, vals_words, vals_scales, base, offs2, offs, out):
    nc = tc.nc
    halves = [slice(0, HALF), slice(HALF, SLOTS)]
    list_halves = [slice(0, HALF // 16), slice(HALF // 16, SLOTS // 16)]

    with ExitStack() as ctx:
        sb = ctx.enter_context(tc.tile_pool(name="sb", bufs=1))
        psum = ctx.enter_context(tc.psum_pool(name="psum", bufs=1))

        def row(name):
            return sb.tile([P, SLOTS], F32, name=name, align_bytes=64)

        def col(name):
            return sb.tile([P, 1], F32, name=name)

        tokens = sb.tile([P, SLOTS // 16], U16, name="tokens")
        links = sb.tile([P, SLOTS // 16], U16, name="links")
        k_words = sb.tile([P, POOL], U16, name="k_words", align_bytes=64)
        k_bytes = sb.tile([P, POOL], U8, name="k_bytes", tag="second", align_bytes=64)
        v_bytes = sb.tile([P, POOL], U8, name="v_bytes", align_bytes=64)
        q_raw = sb.tile([P, PACK, P], F32, name="q_raw", tag="first", align_bytes=64)
        res = col("res")

        def load_bytes(tile, scales):
            for quad in range(4):
                nc.sync.dma_start(tile[32 * quad : 32 * quad + 4, :].bitcast(I32), scales[0, 4 * quad : 4 * quad + 4, :].bitcast(I32))

        nc.vector.memset(k_bytes[:].bitcast(I32), 0)
        nc.gpsimd.memset(v_bytes[:].bitcast(I32), 0)
        nc.scalar.dma_start(q_raw[:], query.rearrange("(p j) w -> p j w", j=PACK))
        nc.gpsimd.dma_start(res[:], reserve)
        nc.sync.dma_start(tokens[:], offs)
        nc.sync.dma_start(k_words[:].bitcast(I32), keys_words[0].bitcast(I32))
        load_bytes(k_bytes, keys_scales)
        nc.sync.dma_start(links[:], offs2)
        load_bytes(v_bytes, vals_scales)

        def quantise(name, raw, cast):
            grouped = sb.tile([P, P, PACK], BF16, name=name + "_grouped", align_bytes=64)
            codes = sb.tile([P, P], U32, name=name + "_codes", align_bytes=64)
            plane = sb.tile([P, P], U8, name=name + "_plane", align_bytes=64)
            cast(grouped[:], raw[:].rearrange("p j w -> p w j"))
            nc.vector.quantize_mx(out=codes[:].bitcast(FP8X4), scales=plane[:], in_=grouped[:].rearrange("p w j -> p (w j)"))
            return codes, plane

        def pick(name, window, dtype, tag):
            picked = sb.tile([P, SLOTS], dtype, name=name, tag=tag, align_bytes=64)
            nc.vector.tensor_copy(picked[:], window[:].indirect(tokens[:]))
            return picked

        def product(name, codes, plane, words, scale_bytes):
            acc = psum.tile([P, SLOTS], F32, name=name)
            nc.tensor.matmul_mx(out=acc[:], lhsT=codes[:].bitcast(FP8X4), lhsT_scale=plane[:], rhs=words[:].bitcast(FP4X4), rhs_scale=scale_bytes[:], start=True, stop=True)
            return acc

        lo, hi = halves
        list_lo, list_hi = list_halves
        kb = pick("kb", k_bytes, U8, "kb")
        g_raw = sb.tile([P, PACK, P], F32, name="g_raw", tag="second", align_bytes=64)
        q_codes, q_plane = quantise("q", q_raw, nc.scalar.copy)
        v_words = sb.tile([P, POOL], U16, name="v_words", tag="first", align_bytes=64)
        nc.sync.dma_start(v_words[:].bitcast(I32), vals_words[0].bitcast(I32))
        nc.sync.dma_start(g_raw[:], gout.rearrange("(p j) w -> p j w", j=PACK))
        kw = pick("kw", k_words, U16, "kw")
        a = product("a", q_codes, q_plane, kw, kb)
        p, p_twin = row("p"), row("p_twin")
        z, sz = col("z"), col("sz")
        nc.scalar.activation(p[:], a[:], ACT.Exp, accum_out=z[:])
        nc.scalar.activation(p_twin[:], a[:], ACT.Exp)
        nc.scalar.activation(sz[:], z[:], ACT.Abs_reciprocal_sqrt)
        vb = pick("vb", v_bytes, U8, "vb")
        vw = pick("vw", v_words, U16, "vw")
        g_codes, g_plane = quantise("g", g_raw, nc.vector.tensor_copy)
        c = product("c", g_codes, g_plane, vw, vb)
        base_sb = sb.tile([P, SLOTS], F32, name="base_sb", tag="second", align_bytes=64)
        nc.sync.dma_start(base_sb[:], base)

        n = sb.tile([P, SLOTS], F32, name="n", tag="first", align_bytes=64)
        u = row("u")
        s = sb.tile([P, HALF], F32, name="s", align_bytes=64)
        for h, lh in zip(halves, list_halves):
            nc.vector.tensor_tensor(n[:, h], p[:].indirect(links[:, lh]), p_twin[:, h], ADD)
        niz = sb.tile([P, 1], F32, name="niz", tag="p_twin", align_bytes=64)
        nc.vector.tensor_scalar(niz[:], sz[:], sz[:], -1.0, MULT, MULT)
        for h in halves:
            nc.scalar.activation(s[:], n[:, h], ACT.Abs_reciprocal_sqrt, bias=res[:])
            nc.scalar.activation(u[:, h], s[:], ACT.Square)
        p2 = sb.tile([P, SLOTS], F32, name="p2", tag="s", align_bytes=64)
        nc.scalar.activation(p2[:], p[:], ACT.Square)

        r, apn, na, e1, s1 = row("r"), row("apn"), row("na"), row("e1"), row("s1")
        m, jn = row("m"), row("jn")
        sn = [col("sn0"), col("sn1")]
        ndz = col("ndz")
        nc.vector.tensor_tensor(r[:, lo], p[:, lo], u[:, lo], MULT)
        nc.vector.scalar_tensor_tensor(na[:, lo], c[:, lo], niz[:], r[:, lo], MULT, MULT)
        nc.vector.tensor_tensor(e1[:, lo], na[:, lo], r[:, lo], MULT)
        nc.scalar.activation(s1[:].indirect(links[:, list_lo]), e1[:, lo], ACT.Copy)
        nc.vector.tensor_tensor(r[:, hi], p[:, hi], u[:, hi], MULT)
        nc.vector.scalar_tensor_tensor(apn[:, lo], na[:, lo], 1.0, p[:, lo], MULT, MULT, accum_out=sn[0][:])
        nc.vector.scalar_tensor_tensor(na[:, hi], c[:, hi], niz[:], r[:, hi], MULT, MULT)
        nc.vector.scalar_tensor_tensor(m[:, lo], na[:, lo], -2.0, e1[:, lo], MULT, ADD)
        nc.vector.tensor_tensor(e1[:, hi], na[:, hi], r[:, hi], MULT)
        nc.scalar.activation(s1[:].indirect(links[:, list_hi]), e1[:, hi], ACT.Copy)
        nc.vector.scalar_tensor_tensor(apn[:, hi], na[:, hi], 1.0, p[:, hi], MULT, MULT, accum_out=sn[1][:])
        nc.vector.scalar_tensor_tensor(m[:, hi], na[:, hi], -2.0, e1[:, hi], MULT, ADD)
        nc.vector.tensor_scalar(ndz[:], sn[0][:], sn[1][:], niz[:], ADD, MULT)
        nc.vector.tensor_tensor(jn[:], na[:], e1[:], SUB)

        dp = na
        hdp, hh = row("hdp"), row("hh")
        hsum = [col("hsum0"), col("hsum1")]
        for h in halves:
            nc.vector.scalar_tensor_tensor(dp[:, h], s1[:, h], ndz[:], m[:, h], SUB, ADD)
        for h, acc in zip(halves, hsum):
            nc.vector.scalar_tensor_tensor(hdp[:, h], dp[:, h], PENALTY, p2[:, h], MULT, MULT, accum_out=acc[:])

        he1, y, y2, zz, f, e5, s5 = row("he1"), row("y"), row("y2"), row("zz"), row("f"), row("e5"), row("s5")
        g1, g2, g3, g4, y_out = row("g1"), row("g2"), row("g3"), row("g4"), row("y_out")
        nbeta, sh, w, hz = col("nbeta"), col("sh"), col("w"), col("hz")
        for h, lh in zip(halves, list_halves):
            nc.scalar.activation(he1[:, h], hdp[:].indirect(links[:, lh]), ACT.Copy)
        nc.vector.scalar_tensor_tensor(y[:, lo], hdp[:, lo], 2.0, jn[:, lo], MULT, MULT)
        nc.vector.tensor_scalar(nbeta[:], hsum[0][:], hsum[1][:], niz[:], ADD, MULT)
        nc.vector.scalar_tensor_tensor(y[:, hi], hdp[:, hi], 2.0, jn[:, hi], MULT, MULT)
        nc.vector.scalar_tensor_tensor(y2[:, lo], apn[:, lo], nbeta[:], y[:, lo], MULT, ADD)
        nc.vector.scalar_tensor_tensor(zz[:, lo], he1[:, lo], 2.0, e1[:, lo], MULT, MULT)
        nc.vector.scalar_tensor_tensor(y2[:, hi], apn[:, hi], nbeta[:], y[:, hi], MULT, ADD)
        nc.vector.tensor_tensor(f[:, lo], y2[:, lo], zz[:, lo], SUB)
        nc.vector.scalar_tensor_tensor(zz[:, hi], he1[:, hi], 2.0, e1[:, hi], MULT, MULT)
        nc.vector.tensor_tensor(e5[:, lo], f[:, lo], u[:, lo], MULT)
        nc.scalar.activation(s5[:].indirect(links[:, list_lo]), e5[:, lo], ACT.Copy)
        nc.vector.tensor_tensor(f[:, hi], y2[:, hi], zz[:, hi], SUB)
        nc.vector.scalar_tensor_tensor(g1[:, lo], apn[:, lo], nbeta[:], base_sb[:, lo], MULT, SUB)
        nc.vector.tensor_tensor(e5[:, hi], f[:, hi], u[:, hi], MULT)
        nc.scalar.activation(s5[:].indirect(links[:, list_hi]), e5[:, hi], ACT.Copy)
        nc.vector.scalar_tensor_tensor(hh[:], hdp[:], 1.0, dp[:], MULT, MULT, accum_out=sh[:])
        nc.vector.scalar_tensor_tensor(g1[:, hi], apn[:, hi], nbeta[:], base_sb[:, hi], MULT, SUB)
        nc.vector.tensor_scalar(w[:], nbeta[:], ndz[:], None, MULT)
        nc.vector.scalar_tensor_tensor(g2[:], r[:], 1.0, f[:], SUB, MULT)
        nc.vector.tensor_tensor(g3[:], g1[:], hh[:], SUB)
        nc.vector.tensor_scalar(hz[:], sh[:], niz[:], w[:], MULT, SUB)
        for h in halves:
            nc.vector.tensor_tensor(g4[:, h], g2[:, h], g3[:, h], SUB)
        t = g2
        for h in halves:
            nc.vector.scalar_tensor_tensor(t[:, h], s5[:, h], hz[:], p[:, h], ADD, MULT)
        for h in halves:
            nc.vector.tensor_tensor(y_out[:, h], t[:, h], g4[:, h], ADD)
            nc.sync.dma_start(out[:, h], y_out[:, h])
